import numpy as np, ml_dtypes
CORES = [3,11,19,27,35,43,51,59]
N = 8
BF = ml_dtypes.bfloat16
def gentries(a):
    return np.ascontiguousarray(a.reshape(8, 16, -1).transpose(0, 2, 1)).reshape(8, -1)
def gtable(e):
    e = np.asarray(e); return np.ascontiguousarray(e.reshape(8, -1, 16).transpose(0, 2, 1)).reshape(128, -1).astype(np.int32)
L, CAP, S, RO, PA = 1536, 256, 64, 2, 3
V = L + RO * CAP; W = V + (N - 1) * 2 * S + 1; NONE = W - 1
G8 = np.arange(8)[:, None]
ARR = np.concatenate([V + (d - 1) * 2 * S + np.arange(S) for d in range(1, N)])
def columns(x):
    return np.ascontiguousarray(x.reshape(N, 8, 16, -1).transpose(0, 1, 3, 2))
def flat(x):
    return np.ascontiguousarray(x.transpose(0, 1, 3, 2)).reshape(N, 128, -1)
def slots(rng, n, share):
    e = rng.integers(0, L, (N, 8, L, 16)); far = ARR[rng.integers(0, len(ARR), e.shape)]
    e = np.where(rng.random(e.shape) < share, far, e)
    return np.where(np.argsort(rng.random(e.shape), axis=-1) < n, e, NONE)
def showing(rng):
    return np.ascontiguousarray(np.argsort(rng.random((N, 8, N - 1, L)), axis=-1)[..., :S])
def pack(e, v, th, sh):
    return {"e": flat(e).astype(np.int32), "v0": flat(v).astype(np.float32).astype(BF), "th": np.ascontiguousarray(np.repeat(th, 16, axis=1)[:, :, None]).astype(np.int32),
            "sh": np.stack([gtable(a.reshape(8, -1)) for a in sh])}
def setup_inputs(rng):
    e = slots(rng, rng.integers(6, 17, (N, 8, L, 1)), 0.3)
    v = (256 * (0.25 + 0.75 * rng.random((N, 8, L, 1))) * rng.random((N, 8, L, 16))).astype(np.int64)
    base = np.array([120, 250, 400, 550, 700, 900, 1100, 1400])
    th = base[np.argsort(rng.random((N, 8)), axis=1)] + rng.integers(-50, 51, (N, 8))
    return pack(e, v, th, showing(rng))
def setup_inputs_room(rng):
    e = slots(rng, rng.integers(15, 17, (N, 8, L, 1)), 0.3)
    n = rng.choice(np.array([0, 1, CAP - 1, CAP, CAP + 1, L]), (N, 8)); n[0] = [CAP, CAP + 1, L, CAP - 1, 1, 0, CAP, CAP + 1]
    hot = np.argsort(rng.random((N, 8, L)), axis=-1) < n[:, :, None]; hot[0, 4] = False; hot[0, 4, L - 1] = True
    v = np.where(hot[..., None], rng.integers(200, 256, (N, 8, L, 16)), rng.integers(136, 200, (N, 8, L, 16)))
    return pack(e, v, np.full((N, 8), 3200), showing(rng))
def setup_inputs_ties(rng):
    e = slots(rng, rng.choice(np.array([8, 10, 12, 16]), (N, 8, L, 1)), 0.3)
    base = rng.integers(8, 128, (1, 8, 1, 16)); kind = rng.integers(1, 3, (N, 8, L, 1)); kind[:, ::2] = 2
    add = rng.integers(0, 2, (N, 8)); add[0] = 0; add[1, ::2] = 1
    th = np.sum(base, axis=-1)[..., 0] * np.where(np.arange(8) % 2 == 0, 2, 1)[None, :] + add
    return pack(e, base * kind, th, showing(rng))
def setup_inputs_ends(rng):
    e = slots(rng, rng.integers(10, 17, (N, 8, L, 1)), 0.3); v = rng.integers(60, 256, (N, 8, L, 16)); sh = showing(rng)
    e[:, 0] = rng.choice(np.array([0, L - 1, L, V - 1, V, V + S - 1, V + S, W - 2, NONE]), (N, L, 16))
    e[:, 1] = rng.integers(0, W, (N, L, 16)); e[:, 2] = ARR[rng.integers(0, len(ARR), (N, L, 16))]; e[:, 3] = rng.integers(0, L, (N, L, 16))
    e[:, 4] = rng.integers(0, L, (N, L, 1)); e[:, 4, :, 9] = NONE
    e[:, 5] = np.where(rng.random((N, L, 1)) < 0.3, NONE, e[:, 5])
    sh[:, ::2] = rng.choice(np.array([0, L - 1, L >> 1, 3]), (N, 4, N - 1, S))
    th = rng.choice(np.array([1, 2, 500, 1500]), (N, 8)); th[0, 7] = 4096; th[1, 0] = 1
    return pack(e, v, th, sh)
def setup_inputs_heavy(rng):
    e = slots(rng, rng.integers(0, 4, (N, 8, L, 1)), 0.2); v = rng.integers(1, 32, (N, 8, L, 16))
    o = 8 + np.argsort(rng.random((N, 8, L - 8)), axis=-1)[..., :64]; kind = rng.integers(0, 4, (N, 8, L))
    a = np.take_along_axis(o, rng.integers(0, 64, (N, 8, L)), 2); b = np.take_along_axis(o, rng.integers(0, 64, (N, 8, L)), 2)
    e[..., 0] = np.where((kind == 0) | (kind == 3), a, e[..., 0]); e[..., 15] = np.where((kind == 1) | (kind == 3), b, e[..., 15])
    one = np.arange(16) == rng.integers(0, 16, (N, 8, L, 1))
    e = np.where(kind[..., None] == 2, np.where(one, a[..., None], NONE), e)
    for q in range(N):
        for g in range(8):
            e[q, g, o[q, g]] = rng.choice(o[q, g], (64, 16)); v[q, g, o[q, g]] = 255
    e[:, :, 0] = NONE; v[:, :, :PA + 1] = 200
    for j in range(1, PA + 1): e[:, :, j] = j - 1
    e[:, ::2, PA, 0] = NONE
    th = rng.choice(np.array([1, 150, 250, 4080]), (N, 8)); th[0, 0] = 150; th[1, 3] = 4080; th[2, 5] = 2040; th[3, 3] = 4081; th[:, 6:] = 1
    sh = showing(rng)
    e[:, 6, :, 8:] = np.arange(L)[None, :, None]; v[:, 6] = rng.integers(1, 256, (N, L, 16))
    at = 0
    for r in range(RO):
        m = at + PA * (r + 1); e[:, 6, at] = NONE; v[:, 6, at:m + 1] = 200
        for j in range(at + 1, m + 1): e[:, 6, j] = j - 1
        e[1::2, 6, m, 0] = NONE
        at = m + 1 + CAP
    e[:, 6, PA + 1] = PA + 3; e[:, 6, PA + 1, 0] = PA + 2; v[:, 6, PA + 2] = 250; v[:, 6, PA + 3] = 255
    v[:, 6, L - 16:] = 0; e[:, 6, L - 16:] = NONE; e[:, 6, L - 16:, 3] = PA + 4; e[:, 6, L - 32:L - 16, 5] = np.arange(L - 16, L)
    t0 = (RO - 1) * CAP + 1; pool = np.concatenate([t0 + np.arange(CAP - 1), ARR])
    e[:, 7] = pool[rng.integers(0, len(pool), (N, L, 16))]; e[:, 7, :, 5:11] = NONE
    v[:, 7] = rng.integers(1, 256, (N, L, 16)); v[:, 7, t0:t0 + CAP - 1] = rng.integers(204, 256, (N, CAP - 1, 16))
    sh[:, 7] = t0 + np.argsort(rng.random((N, N - 1, CAP - 1)), axis=-1)[..., :S]; sh[:, 7, 0] = t0 + rng.integers(0, CAP - 1, (N, 1))
    e[:, 7, 0, 0] = ARR[-1]; e[:, 7, 1, 0] = V + S - 1
    e[1, 7, L - 1] = NONE; v[1, 7, L - 1] = 255; sh[1, 7, 1, 0] = L - 1; e[3, 7, 2] = V + 2 * S; v[3, 7, 2] = 255
    return pack(e, v, th, sh)
def setup_inputs_spread(rng):
    e = slots(rng, 16 - (14 * rng.random((N, 8, L, 1)) ** 2).astype(np.int64), 0.3)
    e = np.where((e < L) & (rng.random(e.shape) < 0.7), (L * rng.random(e.shape) ** 3).astype(np.int64), e)
    v = np.minimum((np.exp2(3 + 5 * rng.random((N, 8, L, 1))) * rng.random((N, 8, L, 16))).astype(np.int64), 255)
    th = np.minimum(np.maximum(np.exp2(12 * rng.random((N, 8))).astype(np.int64), 1), 4096); th[:, 2] = np.minimum(th[:, 2], 30)
    return pack(e, v, th, showing(rng))
def check_inputs(d):
    bad = []
    for k, lo, hi in (("e", 0, W - 1), ("th", 1, 4096), ("sh", 0, L - 1)):
        if np.min(d[k]) < lo or np.max(d[k]) > hi: bad.append("range of " + k)
    x = np.asarray(d["v0"]).astype(np.float64)
    if not np.all((x >= 0) & (x <= 255) & (x == np.floor(x))): bad.append("v0 is not whole numbers from 0 to 255")
    t = np.asarray(d["th"]).reshape(N, 8, 16)
    if not np.all(t == t[:, :, :1]): bad.append("th differs inside a group")
    return bad
def reference(e, v0, th, sh):
    E = np.full((N, 8, V, 16), NONE, np.int32); E[:, :, :L] = columns(e)
    v = np.zeros((N, 8, V, 16), np.int32); v[:, :, :L] = columns(v0.astype(np.float32)).astype(np.int32)
    t = th.reshape(N, 8, 16)[:, :, 0].astype(np.int64)
    half = np.full((N, 8, L), V, np.int64)
    sl = np.stack([gentries(a) for a in sh]).astype(np.int64).reshape(N, 8, N - 1, S)
    def show():
        z = np.concatenate([v, np.zeros((N, 8, 1, 16), np.int32)], axis=2); w = np.zeros((N, 8, W, 16), np.int32); w[:, :, :V] = v
        for a in range(N):
            for d in range(1, N):
                q = (a - d) % N; ix = sl[q, :, d - 1]; b = V + (d - 1) * 2 * S
                w[a, :, b:b + S] = z[q][G8, ix]; w[a, :, b + S:b + 2 * S] = z[q][G8, half[q][G8, ix]]
        return w
    for rnd in range(RO):
        for step in range(PA):
            w = show()
            for a in range(N):
                for g in range(8):
                    v[a, g] = np.minimum(v[a, g], np.add.reduce(w[a, g][E[a, g]], axis=1) >> 3)
        w = show(); fresh = np.zeros((N, 8, L), bool); new = np.full((N, 8, W), -1, np.int32)
        for a in range(N):
            for g in range(8):
                s = np.flatnonzero((half[a, g] == V) & (np.add.reduce(v[a, g, :L], axis=1) >= t[a, g]))[:CAP]
                h = L + CAP * rnd + np.arange(len(s)); old = E[a, g, s]
                C = np.add.accumulate(np.add.reduce(w[a, g][old], axis=2), axis=1)
                cut = np.argmax(2 * C >= C[:, 15:], axis=1); behind = np.arange(16)[None, :] > cut[:, None]
                E[a, g, h] = np.where(behind, old, NONE); E[a, g, s] = np.where(behind, NONE, old)
                x = (v[a, g, s] + 1) >> 1; v[a, g, s] = x; v[a, g, h] = x
                half[a, g, s] = h; fresh[a, g, s] = True; new[a, g, s] = h
        for a in range(N):
            for d in range(1, N):
                q = (a - d) % N; ix = sl[q, :, d - 1]; b = V + (d - 1) * 2 * S
                new[a, :, b:b + S] = np.where(fresh[q][G8, ix], b + S + np.arange(S)[None, :], -1)
            for g in range(8):
                n = new[a, g][E[a, g]]; has = n >= 0; empty = E[a, g] == NONE
                i = np.argmax(has, axis=1); m = np.argmax(empty, axis=1); c = np.flatnonzero(np.any(has, axis=1) & np.any(empty, axis=1))
                E[a, g, c, m[c]] = n[c, i[c]]
    return {"ye": flat(E).astype(np.float32), "yv": flat(v).astype(np.float32).astype(BF)}

from concourse.bass import DstId, RemoteDMATransfer
from concourse.mybir import AluOpType, AxisListType, ActivationFunctionType

L, CAP, SH, N = 1536, 256, 64, 8
V = L + 2 * CAP
NONE = V + (N - 1) * 2 * SH
MID = V - 1
WW = NONE + 16
HV = L + CAP
OFF = {"w0": 0, "w1": 0, "w2": HV}
NG = 5
NE = 6
CM = 384
CQ = 320

C0 = (384, 384, 304, 208, 128, 80, 48)
C1 = (384, 384, 384, 288, 176, 112, 64)
C5 = (256, 320, 320, 320, 256, 192, 128)
C9 = (256, 320, 320, 320, 320, 256, 192, 64)
F0 = (0.46,)
F3 = (0.46, 0.46, 0.46, 0.2, 0.1, 0.3, 0.4)
F7 = (0.46, 0.46, 0.46, 0.15, 0.3, 0.1, 0.2)
F5 = (0.42, 0.42, 0.4, 0.3, 0.1, 0.0, 0.0)
F9 = (0.4, 0.4, 0.4, 0.4, 0.35, 0.2, 0.0, 0.0)
FW = 0.4

SCRATCH = {
    "w0": ("sbuf", [128, WW], "bfloat16"),
    "w1": ("sbuf", [128, WW], "bfloat16"),
    "w2": ("sbuf", [128, HV + WW], "bfloat16"),
    "ee": ("sbuf", [128, L], "int32"),
    "ed": ("sbuf", [128, V], "float32"),
    "el": ("sbuf", [128, V], "uint16"),
    "ec": ("sbuf", [128, V], "float16"),
    "fe": ("sbuf", [128, V], "bfloat16"),
    "emp": ("sbuf", [128, 2 * CQ], "bfloat16"),
    "ti": ("sbuf", [128, 2 * CM], "int32"),
    "shi": ("sbuf", [128, 28], "int32"),
    "sl": ("sbuf", [128, 28], "uint16"),
    "sl2": ("sbuf", [128, 28], "uint16"),
    "sl5": ("sbuf", [128, 56], "uint16"),
    "sl6": ("sbuf", [128, 56], "uint16"),
    "sb0": ("sbuf", [128, 896], "bfloat16"),
    "sb1": ("sbuf", [128, 896], "bfloat16"),
    "thi": ("sbuf", [128, 1], "int32"),
    "thf": ("sbuf", [128, 1], "float32"),
    "ones": ("sbuf", [128, CM], "bfloat16"),
    "basec": ("sbuf", [128, 96], "float32"),
    "zz": ("sbuf", [128, 96], "float32"),
    "iotac": ("sbuf", [128, V], "float32"),
    "thr": ("sbuf", [128, 1], "float32"),
    "cand": ("sbuf", [128, 96], "bfloat16"),
    "splt": ("sbuf", [128, 96], "bfloat16"),
    "pfx": ("sbuf", [128, 96], "float32"),
    "rk": ("sbuf", [128, 96], "float32"),
    "of": ("sbuf", [128, 96], "float32"),
    "ofu": ("sbuf", [128, 96], "uint16"),
    "self": ("sbuf", [128, 2 * L], "float32"),
    "selh": ("sbuf", [128, 256], "float16"),
    "sel": ("sbuf", [128, 32], "uint16"),
    "xi": ("sbuf", [128, 256], "int32"),
    "px": ("sbuf", [128, 512], "bfloat16"),
    "neg": ("sbuf", [128, 256], "bfloat16"),
    "dd": ("sbuf", [128, 256], "float32"),
    "dl": ("sbuf", [128, 256], "uint16"),
    "beh": ("sbuf", [128, 256], "float32"),
    "mm_": ("sbuf", [128, 256], "float32"),
    "newd": ("sbuf", [128, WW], "float32"),
    "hb": ("sbuf", [128, 448], "float16"),
    "tl0": ("sbuf", [128, 32], "uint16"),
    "tl1": ("sbuf", [128, 32], "uint16"),
    "yo": ("sbuf", [128, V], "float32"),
}
for _n in ("ga", "gm", "ii", "i8", "dc", "up", "tri", "lo", "lm", "o32", "d8k", "i2", "ith"):
    SCRATCH[_n] = ("sbuf", [128, 128], "bfloat16")
for _n in ("bk", "mka", "mkb", "mk", "aka", "akb", "ak"):
    SCRATCH[_n] = ("sbuf", [128, 2048], "bfloat16")
for _n in ("pi", "pj", "pb"):
    SCRATCH[_n] = ("sbuf", [128, 96], "int32")
for _k in range(NG):
    SCRATCH["g%d" % _k] = ("sbuf", [128, 16 * CM], "bfloat16")
for _k in range(2):
    for _n, _t in (("f", "bfloat16"), ("ff", "bfloat16"), ("x", "float16"), ("gp", "bfloat16"), ("pr", "float16")):
        SCRATCH["%s%d" % (_n, _k)] = ("sbuf", [128, CQ], _t)
for _k in range(8):
    SCRATCH["ps%d" % _k] = ("psum", [128, 512], "float32")

SEMAPHORES = ["qv", "qs", "qt", "qg"] + ["ar%d" % k for k in range(1, 10)] + ["sn%d" % k for k in range(1, 10)] + ["ld%d" % k for k in range(30)]

A = AluOpType
COPY = ActivationFunctionType.Copy
IDENT = ActivationFunctionType.Identity
SIGM = ActivationFunctionType.Sigmoid
SEMQ = {"v": "qv", "s": "qs", "t": "qt", "g": "qg"}


def rank_program(g, core, T, topo):
    rank = T.rank_of(core)
    if rank is None:
        return
    eng = {"v": g.vector, "s": g.scalar, "t": g.tensor, "g": g, "y": g.sync}

    cnt = {"qv": 0, "qs": 0, "qt": 0, "qg": 0}
    know = {q: {} for q in eng}
    acc = {}
    total = {}
    ndma = [0]

    def need(q, tok):
        sem, val, snap = tok
        if know[q].get(sem, 0) >= val:
            return
        eng[q].wait_ge(T.sem[sem], val)
        for s_, v_ in snap.items():
            if know[q].get(s_, 0) < v_:
                know[q][s_] = v_
        know[q][sem] = val

    def deps(q, reads, writes):
        best = {}
        for lst, wr in ((reads, False), (writes, True)):
            for b, a0, a1 in lst:
                ps = b[:2] == "ps"
                for (c0, c1, kind, tok, q2) in acc.get(b, ()):
                    if ps:
                        if q2 == q and (q == "t" or not (wr or kind)):
                            continue
                        if q2 == q and (c0 >= a1 or a0 >= c1):
                            continue
                    elif c0 >= a1 or a0 >= c1 or not (wr or kind):
                        continue
                    if tok[0] not in best or best[tok[0]][1] < tok[1]:
                        best[tok[0]] = tok
        for t in sorted(best.values(), key=lambda t: -len(t[2])):
            need(q, t)

    def note(q, tok, reads, writes):
        for lst, kind in ((writes, True), (reads, False)):
            for b, a0, a1 in lst:
                keep = []
                for e in acc.get(b, []):
                    inside = a0 <= e[0] and e[1] <= a1
                    if inside and (kind or (not e[2] and e[4] == q)):
                        continue
                    keep.append(e)
                keep.append((a0, a1, kind, tok, q))
                acc[b] = keep

    def iv(s):
        if s[0] == "ind":
            return iv(s[1]) + iv(s[2])
        return [(s[0], s[1], s[2])]

    def ap(s):
        if s[0] == "ind":
            return ap(s[1]).indirect(ap(s[2]))
        if len(s) == 4:
            return T[s[0]][:, s[1]:s[2]:s[3]]
        return T[s[0]][:, s[1]:s[2]]

    def emit(q, out, ins, fn):
        reads, writes = [], []
        for s in ins:
            reads += iv(s)
        if out[0] == "ind":
            writes += iv(out[1])
            reads += iv(out[2])
        else:
            writes += iv(out)
        deps(q, reads, writes)
        sem = SEMQ[q]
        snap = dict(know[q])
        fn(eng[q]).then_inc(T.sem[sem], 1)
        cnt[sem] += 1
        total[sem] = cnt[sem]
        note(q, (sem, cnt[sem], snap), reads, writes)

    def ind(win, off):
        return ("ind", win, off)

    def vcopy(o, i):
        emit("v", o, [i], lambda e: e.tensor_copy(ap(o), ap(i)))

    def vtt(o, i0, i1, op):
        emit("v", o, [i0, i1], lambda e: e.tensor_tensor(ap(o), ap(i0), ap(i1), op))

    def vts(o, i0, s1, op0, s2=None, op1=None):
        col = isinstance(s1, tuple)
        a1 = ap(s1) if col else s1
        ins = [i0, s1] if col else [i0]
        if op1 is None:
            emit("v", o, ins, lambda e: e.tensor_scalar(ap(o), ap(i0), a1, None, op0))
        else:
            emit("v", o, ins, lambda e: e.tensor_scalar(ap(o), ap(i0), a1, s2, op0, op1))

    def mset(o, c):
        emit("v", o, [], lambda e: e.memset(ap(o), c))

    def act(o, i, bias=0.0):
        if bias == 0.0:
            emit("s", o, [i], lambda e: e.activation(ap(o), ap(i), COPY))
        else:
            emit("s", o, [i], lambda e: e.activation(ap(o), ap(i), IDENT, bias, 1.0))

    def step(o, i, bias, scale):
        emit("s", o, [i], lambda e: e.activation(ap(o), ap(i), SIGM, bias, scale))

    def mm(o, l, r, start, stop):
        emit("t", o, [l, r], lambda e: e.matmul(ap(o), ap(l), ap(r), start, stop))

    def asel(o, i, pat, op, fill, base, cm):
        emit("g", o, [i], lambda e: e.affine_select(ap(o), ap(i), pat, op, fill, base, cm))

    def iota(o, pat, base, cm, small=False):
        if small:
            emit("g", o, [], lambda e: e.iota(ap(o), pat, base, cm, allow_small_or_imprecise_dtypes=True))
        else:
            emit("g", o, [], lambda e: e.iota(ap(o), pat, base, cm))

    def dma(q, o_ap, i_ap, outs, ins):
        deps(q, ins, outs)
        sem = "ld%d" % ndma[0]
        ndma[0] += 1
        snap = dict(know[q])
        eng[q].dma_start(o_ap, i_ap).then_inc(T.sem[sem], 16)
        total[sem] = 16
        note("d", (sem, 16, snap), ins, outs)

    def wb(k):
        return "w%d" % (k % 3)

    def col(w, a, b):
        return (w, OFF[w] + a, OFF[w] + b)

    def blk(m, i):
        return (m, 128 * i, 128 * i + 128)

    def sq(m):
        return (m, 0, 128)

    def show(k, src, lst, width, share=0.5):
        n = 7 * width
        lc = n // 16
        h = int(lc * share) // 2 * 2
        sb = "sb%d" % (k % 2)
        vcopy((sb, 0, h * 16), ind(src, (lst, 0, h)))
        act((sb, h * 16, n), ind(src, (lst, h, lc)))
        reads = [(sb, 0, n)]
        deps("g", reads, [])
        tr, land = [], []
        for d in range(1, N):
            dst = T.cores[(rank + d) % N]
            a = topo.addr(dst)
            e = topo.engines(core, dst)[d - 1]
            b = V + (d - 1) * 2 * SH
            spot = col(wb(k), b, b + width)
            land.append(spot)
            tr.append(RemoteDMATransfer(dst_ids=[DstId(rid=a[0], pnc=a[1])], dma_engine_mask=1 << e, remote_sem=T.sem["ar%d" % k],
                                        src=T[sb][:, (d - 1) * width:d * width], dst=ap(spot)))
        g.remote_dma_fused(tr, local_sem=T.sem["sn%d" % k])
        total["sn%d" % k] = 7
        total["ar%d" % k] = 7
        note("r", ("sn%d" % k, 7, dict(know["g"])), reads, [])
        for spot in land:
            note("r", ("ar%d" % k, 7, {}), [], [spot])

    gi = [0]

    def even(x):
        return int(x) // 2 * 2

    def at(f, i):
        return f[min(i, len(f) - 1)]

    def chunks(sizes):
        res, a = [], 0
        for s in sizes:
            res.append((a, a + s))
            a += s
        return res

    def gather(k, a, b, fv, parts=1):
        G = "g%d" % (gi[0] % NG)
        gi[0] += 1
        w = b - a
        v = even(w * fv + 1)
        win = col(wb(k), 0, WW)
        cuts = [even(v * i / parts) for i in range(parts)] + [v]
        act((G, 16 * v, 16 * w), ind(win, ("el", a + v, b)))

        def part(i):
            p, q = cuts[i], cuts[i + 1]
            if q > p:
                vcopy((G, 16 * p, 16 * q), ind(win, ("el", a + p, a + q)))
        if parts == 1:
            part(0)
        return G, part

    def sums(G, ps, w, const):
        if const:
            mm((ps, 0, w), sq("dc"), ("ones", 0, w), True, False)
        for i in range(16):
            mm((ps, 0, w), sq("i8"), (G, i, 16 * w, 16), i == 0 and not const, i == 15 and const)

    def mins(ps, old, new, a, b, par):
        w = b - a
        o = CM * (par % 2)
        vtt(("ti", o, o + w), (ps, 0, w), col(old, a, b), A.min)
        vcopy(col(new, a, b), ("ti", o, o + w))

    def clip(k, sizes, fv, hook=None):
        ch = chunks(sizes)
        M = len(ch)
        for i in range(M + 1):
            if i < M:
                G, _p = gather(k, ch[i][0], ch[i][1], at(fv, i))
            if i:
                mins("ps%d" % ((i - 1) % 4), wb(k), wb(k + 1), ch[i - 1][0], ch[i - 1][1], i - 1)
            if i < M:
                if hook:
                    hook(i)
                sums(G, "ps%d" % (i % 4), ch[i][1] - ch[i][0], True)

    def sel_piece(r, w, a, b):
        m0, m1 = a // 16, b // 16
        nm = m1 - m0
        for k in range(16):
            mm(("ps4", 0, nm), blk("bk", k), col(w, a + k, b) + (16,), k == 0, k == 15 and r == 0)
        if r:
            mm(("ps4", 0, nm), sq("d8k"), ("splt", m0, m1), False, True)
        vts(("cand", m0, m1), ("ps4", 0, nm), ("thf", 0, 1), A.is_ge)
        mm(("ps6", 0, nm), sq("gm"), ("cand", m0, m1), True, True)
        mm(("ps5", 0, nm), sq("lm"), ("cand", m0, m1), True, True)
        init = ("pfx", m0 - 1, m0)
        ini = ap(init) if a else 8191.0
        emit("v", ("pfx", m0, m1), [("ps6", 0, nm), ("zz", m0, m1)] + ([init] if a else []),
             lambda e: e.tensor_tensor_scan(ap(("pfx", m0, m1)), ap(("ps6", 0, nm)), ap(("zz", m0, m1)), ini, A.add, A.add))
        vtt(("rk", m0, m1), ("ps5", 0, nm), ("pfx", m0, m1), A.add)
        vtt(("of", m0, m1), ("rk", m0, m1), ("basec", m0, m1), A.min)
        vcopy(("ofu", m0, m1), ("of", m0, m1))
        vcopy(ind(("self", 0, 2 * L), ("ofu", m0, m1)), ("iotac", a, b))

    S16 = ("sel", 0, 16)

    def sel_list(r):
        vcopy(("selh", 0, 256), ("self", 0, 256))
        for k in range(16):
            mm(("ps7", 0, 16), blk("bk", k), ("selh", k, 256, 16), k == 0, k == 15)
        vts(S16, ("ps7", 0, 16), 0.0625, A.mult, 0.0, A.add)
        if r == 0:
            vts(("sel", 16, 32), ("ps7", 0, 16), 0.0625, A.mult, float(HV), A.add)

    def split(r, k):
        w = wb(k)
        h0 = L + CAP * r
        for q in range(2):
            o = 128 * q
            vs = even(128 * FW)
            act(("g%d" % q, 16 * vs, 2048), ind(col(w, 0, WW), ("dl", o + vs, o + 128)))
            vcopy(("g%d" % q, 0, 16 * vs), ind(col(w, 0, WW), ("dl", o, o + vs)))
            for i in range(16):
                mm(("ps6", o, o + 128), blk("ak", i), ("g%d" % q, i, 2048, 16), i == 0, i == 15)
        vts(ind(("newd", 0, V), S16), ("iotac", h0, h0 + CAP), 1.0, A.mult, -float(NONE), A.add)
        mset(("newd", V - 8, V), 0.0)
        vcopy(ind(col(w, 0, V), S16), ("px", 0, 256))
        vcopy(col(w, h0, h0 + CAP), ("px", 0, 256))
        vts(("beh", 0, 256), ("ps6", 0, 256), ("thr", 0, 1), A.is_ge)
        vtt(("mm_", 0, 256), ("beh", 0, 256), ("dd", 0, 256), A.mult)
        vtt(ind(("ed", 0, V), S16), ("dd", 0, 256), ("mm_", 0, 256), A.subtract)
        act(("ed", h0, h0 + CAP), ("mm_", 0, 256))

    def pointer_pass(k, sizes, fv, last, hook=None):
        ch = chunks(sizes)
        M = len(ch)
        old, new = wb(k - 1), wb(k + 1)
        win = col(wb(k), 0, WW)
        Gs = {}

        def sb(j):
            return "ps%d" % (j % 4)

        def xb(j):
            return ("ps4" if j % 2 else "ps5") if last else "ps5"

        def prep(i):
            a, b = ch[i]
            vts(("el", a, b), ("ed", a, b), float(NONE), A.add)
            Gs[i] = gather(k, a, b, at(fv, i), 2)

        def empties(i):
            a, b = ch[i]
            w = b - a
            o = CQ * (i % 2)
            vts(("emp", o, o + w), ("el", a, b), float(NONE), A.is_equal)
            vts(("ec", a, b), ("el", a, b), float(MID), A.subtract)
            mm(("ps6", 64, 64 + w), sq("tri"), ("emp", o, o + w), True, True)
            vts(("fe", a, b), ("ps6", 64, 64 + w), 1.0, A.is_ge)

        prep(0)
        prep(1)
        Gs[0][1](0)
        Gs[0][1](1)
        empties(0)
        for i in range(M + 3):
            n0, n1, n2, n3 = i < M, 0 <= i - 1 < M, 0 <= i - 2 < M, 0 <= i - 3 < M
            late = i >= M if last else i + 2 >= M
            if n0:
                w = ch[i][1] - ch[i][0]
                G = Gs[i][0]
            if n1:
                a1, b1 = ch[i - 1]
                w1 = b1 - a1
                p1 = (i - 1) % 2
                f, ff, x = "f%d" % p1, "ff%d" % p1, "x%d" % p1
            if n2:
                a2, b2 = ch[i - 2]
                w2 = b2 - a2
                p2 = i % 2
                tl, gp, pr = "tl%d" % p2, "gp%d" % p2, "pr%d" % p2
            if n3:
                a3, b3 = ch[i - 3]
                w3 = b3 - a3
                mm(("ps7", 0, w3), sq("ii"), ("ec", a3, b3), True, False)
                mm(("ps7", 0, w3), sq("ii"), ("pr%d" % ((i - 3) % 2), 0, w3), False, True)
                if last:
                    act(("yo", a3, b3), ("ps7", 0, w3), bias=float(MID))
                    dma("y", T.ye[:, a3:b3], T.yo[:, a3:b3], [], [("yo", a3, b3)])
                else:
                    act(("ed", a3, b3), ("ps7", 0, w3), bias=float(MID - NONE))
                    mm((sb(i - 3), 0, w3), sq("dc"), ("ones", 0, w3), False, False)
                    mm((sb(i - 3), 0, w3), sq("i8"), ("gp%d" % ((i - 3) % 2), 0, w3), False, True)
            if n0 and not last:
                sums(G, sb(i), w, False)
            if n1 and not last:
                if late:
                    step((f, 0, w1), ("ps4", 0, w1), -128.0, -1.0)
                else:
                    vts((f, 0, w1), ("ps4", 0, w1), 0.0, A.is_lt)
                mm(("ps5", 0, w1), sq("tri"), (f, 0, w1), True, False)
                mm(("ps5", 0, w1), sq("gm"), ("fe", a1, b1), False, True)
                mm((sb(i - 1), 0, w1), sq("o32"), (f, 0, w1), False, False)
            if i + 1 < M:
                Gs[i + 1][1](0)
            if n2:
                vts((tl, 0, w2 // 16), ("ps6", 0, w2 // 16), float(MID), A.add)
                if not last:
                    act((gp, 0, w2), ind(win, (tl, 0, w2 // 16)))
            if i + 2 < M:
                prep(i + 2)
            if i + 1 < M:
                empties(i + 1)
            if n0 and last:
                mm((xb(i), 0, w), sq("gm"), ("fe", ch[i][0], ch[i][1]), True, False)
                for q in range(16):
                    mm((xb(i), 0, w), blk("mk", q), (G, q, 16 * w, 16), False, q == 15)
            if n1:
                if late:
                    step((ff, 0, w1), (xb(i - 1), 0, w1), -300.0, 200.0)
                else:
                    vts((ff, 0, w1), (xb(i - 1), 0, w1), 2.0, A.is_ge)
                vtt((x, 0, w1), (ff, 0, w1), ("ec", a1, b1), A.mult)
            if n0 and not last:
                for q in range(16):
                    mm(("ps4", 0, w), blk("bk", q), (G, q, 16 * w, 16), q == 0, q == 15)
            if n1:
                for q in range(16):
                    mm(("ps6", 0, w1 // 16), blk("bk", q), (x, q, w1, 16), q == 0, q == 15)
                if not last:
                    mm((sb(i - 1), 0, w1), sq("o32"), (ff, 0, w1), False, False)
            if i + 1 < M:
                Gs[i + 1][1](1)
            if n2:
                vtt((pr, 0, w2), ind(("newd", 0, WW), (tl, 0, w2 // 16)), ("fe", a2, b2), A.mult)
            if n3 and not last:
                mins(sb(i - 3), old, new, a3, b3, i - 3)
            if hook:
                hook(i)

    dma("y", T.shi[:, :], T.sh[:, :], [("shi", 0, 28)], [])
    dma("y", T.w1[:, 0:L // 2], T.v0[:, 0:L // 2], [("w1", 0, L // 2)], [])
    dma("s", T.w1[:, L // 2:L], T.v0[:, L // 2:L], [("w1", L // 2, L)], [])
    ce = L // NE
    for j in range(NE):
        dma("y", T.ee[:, j * ce:(j + 1) * ce], T.e[:, j * ce:(j + 1) * ce], [("ee", j * ce, (j + 1) * ce)], [])
    dma("y", T.thi[:, :], T.th[:, :], [("thi", 0, 1)], [])

    G8 = [[0, 8], [1, 16]]

    def zero_window(w):
        mset(col(w, L, V), 0.0)
        mset(col(w, NONE, WW), 0.0)
        for d in range(1, N):
            b = V + (d - 1) * 2 * SH + SH
            mset(col(w, b, b + SH), 0.0)

    mset(("ones", 0, CM), 1.0)
    asel(sq("ii"), ("ones", 0, 128), [[-1, 128]], A.is_equal, 0.0, 0, 1)
    asel(sq("ga"), ("ones", 0, 128), [[-16, 8], [0, 16]], A.is_ge, 0.0, 0, 1)
    asel(sq("gm"), sq("ga"), [[16, 8], [0, 16]], A.is_ge, 0.0, 15, -1)
    mset(("w1", L, V), 0.0)
    vcopy(("sl", 0, 28), ("shi", 0, 28))
    show(1, ("w1", 0, V), "sl", SH)
    vts(sq("i8"), sq("ii"), 0.125, A.mult)
    vts(sq("dc"), sq("ii"), -0.4375, A.mult)
    for j in range(NE):
        vcopy(("el", j * ce, (j + 1) * ce), ("ee", j * ce, (j + 1) * ce))
    for w in ("w1", "w2", "w0"):
        zero_window(w)
    mset(("w2", 0, HV), 0.0)
    vcopy(("thf", 0, 1), ("thi", 0, 1))
    mset(("ed", L, V), 0.0)
    mset(("newd", 0, V), 0.0)
    mset(("newd", NONE, WW), 0.0)
    mset(("zz", 0, 96), 0.0)
    mset(("neg", 0, 256), 1.0)
    for k in range(16):
        asel(blk("bk", k), sq("gm"), G8, A.is_equal, 0.0, -k, 0)
    asel(sq("up"), sq("gm"), [[1, 128]], A.is_ge, 0.0, 0, -1)
    asel(sq("lo"), sq("gm"), [[-1, 128]], A.is_gt, 0.0, 0, 1)
    asel(sq("ith"), sq("ii"), G8, A.is_equal, 0.0, 0, 0)
    iota(("iotac", 0, V), [[1, V]], 0, 0, True)
    iota(("newd", V, NONE), [[1, NONE - V]], V + SH - NONE, 0, True)
    iota(("pi", 0, 96), [[0, 96]], 0, 1)
    iota(("pb", 0, 96), [[16, 96]], L, 0)

    clip(1, C0, F0)
    show(2, col("w2", 0, V), "sl", SH)
    for k in range(16):
        asel(blk("aka", k), sq("gm"), G8, A.is_gt, -1.0, -k, 0)
    asel(("akb", 0, 2048), ("aka", 0, 2048), [[0, 16], [-16, 8], [0, 16]], A.is_ge, 0.0, 0, 1)
    asel(("ak", 0, 2048), ("akb", 0, 2048), [[0, 16], [16, 8], [0, 16]], A.is_ge, 0.0, 15, -1)
    for d in range(7):
        vts(("sl5", 8 * d, 8 * d + 4), ("sl", 4 * d, 4 * d + 4), float(HV), A.add)
        vcopy(("sl5", 8 * d + 4, 8 * d + 8), ("sl", 4 * d, 4 * d + 4))
        vcopy(("sl6", 8 * d, 8 * d + 4), ("sl", 4 * d, 4 * d + 4))
    vts(("ed", 0, L), ("ee", 0, L), -float(NONE), A.add)
    vts(sq("d8k"), sq("ii"), -8192.0, A.mult)
    vtt(sq("lm"), sq("d8k"), sq("lo"), A.subtract)
    vts(sq("i2"), sq("ii"), 2.0, A.mult)
    vtt(sq("tri"), sq("i2"), sq("up"), A.subtract)
    vts(sq("o32"), sq("gm"), 32.0, A.mult)
    clip(2, C0, F0)
    show(3, ("w0", 0, V), "sl", SH)
    mset(("mka", 0, 2048), -1.0)
    K3 = [[-1, 16], [0, 8], [1, 16]]
    asel(("mkb", 0, 2048), ("mka", 0, 2048), K3, A.is_gt, 1.0, 0, 0)
    asel(("mka", 0, 2048), ("mkb", 0, 2048), K3, A.is_ge, 0.0, 0, 0)
    asel(("mk", 0, 2048), ("mka", 0, 2048), [[0, 16], [-16, 8], [-1, 16]], A.is_equal, 0.0, 0, 1)
    emit("v", ("thr", 0, 1), [sq("ith")], lambda e: e.tensor_reduce(ap(("thr", 0, 1)), ap(sq("ith")), AxisListType.X, A.add))
    vts(("pj", 0, 96), ("pi", 0, 96), 15, A.bitwise_and)
    vtt(("basec", 0, 96), ("pj", 0, 96), ("pb", 0, 96), A.add)
    vcopy(("self", 0, 256), ("iotac", L, L + CAP))

    c0 = chunks(C0)
    H = 1024

    def hook3(i):
        if i:
            act(col("w2", c0[i - 1][0], c0[i - 1][1]), ("w1", c0[i - 1][0], c0[i - 1][1]))
        if i == 3:
            sel_piece(0, "w1", 0, H)

    clip(3, C0, F3, hook3)
    show(4, ("w1", 0, V), "sl", SH)
    act(col("w2", c0[-1][0], c0[-1][1]), ("w1", c0[-1][0], c0[-1][1]))
    sel_piece(0, "w1", H, L)
    sel_list(0)
    vts(("xi", 0, 256), ind(("w1", 0, V), S16), 0.5, A.mult, 0.25, A.add)
    act(("dd", 0, 256), ind(("ed", 0, V), S16))
    vcopy(("px", 0, 256), ("xi", 0, 256))
    vts(("px", 256, 512), ("xi", 0, 256), -256.0, A.add)
    vcopy(ind(("w2", 0, HV + V), ("sel", 0, 32)), ("px", 0, 512))
    show(5, ("w2", 0, HV + V), "sl5", 2 * SH)
    vts(("dl", 0, 256), ("dd", 0, 256), float(NONE), A.add)
    vcopy(col("w2", L, L + CAP), ("px", 0, 256))
    split(0, 4)

    def hook5(i):
        if i == 2:
            vts(("hb", 0, 448), ind(("newd", 0, V), ("sl", 0, 28)), float(MID - NONE), A.min)
        if i == 3:
            for k in range(16):
                mm(("ps6", 32, 60), blk("bk", k), ("hb", k, 448, 16), k == 0, k == 15)
            for d in range(7):
                vts(("sl6", 8 * d + 4, 8 * d + 8), ("ps6", 32 + 4 * d, 36 + 4 * d), 0.0625, A.mult, float(NONE), A.add)

    pointer_pass(5, C5, F5, False, hook5)
    show(6, ("w0", 0, V), "sl6", 2 * SH)
    for a, b in chunks(C1):
        vts(("el", a, b), ("ed", a, b), float(NONE), A.add)
    vts(("splt", 0, 96), ("of", 0, 96), 256.0, A.is_lt)
    vcopy(("self", 0, 256), ("iotac", L + CAP, L + 2 * CAP))
    clip(6, C1, F0)
    show(7, ("w1", 0, V), "sl6", 2 * SH)
    zero_window("w0")
    mset(("w0", 0, L), 0.0)

    def hook7(i):
        if i == 3:
            sel_piece(1, "w2", 0, H)
        if i == 5:
            sel_piece(1, "w2", H, L)

    clip(7, C1, F7, hook7)
    show(8, col("w2", 0, V), "sl6", 2 * SH, 0.3)
    sel_list(1)
    vcopy(ind(("w0", 0, V), S16), ("neg", 0, 256))
    mset(("w0", L + CAP, V), 0.0)
    show(9, ("w0", 0, V), "sl", SH)
    act(("dd", 0, 256), ind(("ed", 0, V), S16))
    vts(("dl", 0, 256), ("dd", 0, 256), float(NONE), A.add)
    vts(("xi", 0, 256), ind(col("w2", 0, V), S16), 0.5, A.mult, 0.25, A.add)
    vcopy(("px", 0, 256), ("xi", 0, 256))
    split(1, 8)
    dma("y", T.yv[:, :], T.w2[:, HV:HV + V], [], [("w2", HV, HV + V)])
    pointer_pass(9, C9, F9, True)

    for sem in sorted(total):
        if know["y"].get(sem, 0) < total[sem]:
            g.sync.wait_ge(T.sem[sem], total[sem])
